import numpy as np, ml_dtypes
CORES = [25,29,65,69,153,157,193,197]
N = 8
BF = ml_dtypes.bfloat16
def gentries(a):
    return np.ascontiguousarray(a.reshape(8, 16, -1).transpose(0, 2, 1)).reshape(8, -1)
def gtable(e):
    e = np.asarray(e); return np.ascontiguousarray(e.reshape(8, -1, 16).transpose(0, 2, 1)).reshape(128, -1).astype(np.int32)
W, C, RO, K = 2048, 128, 5, 3
M = W - 1
def parts(rng):
    ct = rng.integers(0, W, (N, 8, 16, C)); bk = (16 * rng.random((N, 8, 1, W)) * rng.random((N, 8, 16, W))).astype(np.int64)
    pr = rng.integers(0, 241, (N, 8, 16, C)); pg = rng.integers(0, C, (N, 8, C))
    a = rng.integers(0, W, (N, 8, C)); th = rng.integers(500, 1100, (N, 8, C))
    return ct, bk, pr, pg, a, th
def pack(ct, bk, pr, pg, a, th):
    return {"ct": np.ascontiguousarray(ct.reshape(N, 128, C)).astype(np.int32), "bk": np.ascontiguousarray(bk.reshape(N, 128, W)).astype(np.float32).astype(BF),
            "pr": np.ascontiguousarray(pr.reshape(N, 128, C)).astype(np.int32), "pg": np.stack([gtable(x) for x in pg]), "a0": a.astype(np.int32), "th": th.astype(np.int32)}
def setup_inputs(rng):
    return pack(*parts(rng))
def setup_inputs_ties(rng):
    ct, bk, pr, pg, a, th = parts(rng)
    bk = (rng.random((N, 8, 16, W)) < rng.choice(np.array([0.02, 0.05, 0.1]), (N, 8, 1, 1))).astype(np.int64)
    pr = rng.integers(0, 3, (N, 8, 16, C)); th = rng.integers(0, 20, (N, 8, C))
    pr[:, 1::2] = np.minimum(pr[:, 1::2] + 1, 2)
    bk[:, 0] = rng.integers(1, 5, (N, 16, W)); th[:, 0] = np.add.reduce(pr[:, 0], axis=1) + rng.integers(0, 2, (N, C))
    return pack(ct, bk, pr, pg, a, th)
def setup_inputs_ends(rng):
    ct, bk, pr, pg, a, th = parts(rng); e = np.array([0, 1, W // 2, M - 1, M])
    ct[:, ::2] = e[rng.integers(0, 5, (N, 4, 16, C))]; a[:, ::2] = e[rng.integers(0, 5, (N, 4, C))]
    ct[:, 4, :, ::2] = rng.integers(0, W, (N, 16, C // 2))
    ct[:, 1] = ct[:, 1, :1]
    pg[:, 5] = rng.integers(0, C, (N, 1)); pg[:, 6] = rng.choice(np.array([0, C - 1]), (N, C)); pg[:, 0] = rng.choice(np.array([0, C - 1, 1]), (N, C))
    th = np.where(rng.random(th.shape) < 0.5, th, rng.choice(np.array([0, 4095]), th.shape))
    a[:, 3] = a[:1, 3]; ct[:, 3] = (rng.permutation(W).reshape(16, C) + a[:, 3, None]) & M; pg[:, 3] = np.arange(C); th[:, 3] = 0
    low = int(rng.integers(0, 2)) * (C // 2); dd = low + np.arange(0, C // 2, 2)
    s7 = 16 * (low + 1 + 2 * rng.integers(0, C // 4, (16, C))) + rng.integers(0, 16, (16, C))
    s7[0, dd] = 16 * dd + 1; s7[1, dd] = 16 * dd + 16
    a[:, 7] = a[:1, 7]; ct[:, 7] = (s7 + a[:, 7, None]) & M; pg[:, 7] = np.arange(C); pr[:, 7] = 240
    b7 = bk[:, 7]; b7[:, :, 16 * dd + 1] = rng.integers(9, 16, (N, 16, len(dd))); b7[:, :, 16 * dd + 16] = 0
    v7 = worth(bk[:, 7:8], ((ct - a[:, :, None, :]) & M)[:, 7:8], pr[:, 7:8])[:, 0]
    th[:, 7] = 4095; t7 = th[:, 7]; t7[:, dd] = v7[:, dd] - 16 * rng.integers(0, 2, (N, len(dd)))
    return pack(ct, bk, pr, pg, a, th)
def setup_inputs_full(rng):
    ct, bk, pr, pg, a, th = parts(rng)
    bk[:, ::2] = 15 - rng.integers(0, 4, (N, 4, 16, W)) * (rng.random((N, 4, 16, W)) < 0.1)
    ct[:, 0] &= ~1; a[:, 0] &= ~1
    bk[:, 0, :, 0::2] = 15; bk[:, 0, :, 1::2] = rng.integers(3, 11, (N, 16, W // 2))
    pr[:, ::2] = rng.choice(np.array([240, 240, 239, 238, 232, 225]), (N, 4, 16, C)); pr[:, 0, :, ::2] = 240
    th[:, ::2] = rng.integers(3660, 3820, (N, 4, C)); th[:, 0] = rng.choice(np.array([3800, 3839, 3840, 3841]), (N, C))
    th[:, 0, 0] = 3840; th[:, 0, 2] = 3841
    pr[:, 4, :, 1::2] = 0; th[:, 4, 1::2] = rng.integers(0, 2, (N, C // 2))
    z = W // 4; s1 = rng.integers(0, z, (N, 16, C)); s1[:, 14] = 0; s1[:, 15] = z - 1
    ct[:, 1] = (s1 + a[:, 1, None]) & M; bk[:, 1, :, :z] = 0; bk[:, 1, :, z:] = rng.integers(1, 16, (N, 16, W - z))
    pg[:, 1] = np.argsort(rng.random((N, C)), axis=-1)
    return pack(ct, bk, pr, pg, a, th)
def setup_inputs_crib(rng):
    ct, bk, pr, pg, a, th = parts(rng)
    words = rng.integers(0, W, (8, 16, 4)); plain = np.take_along_axis(words[None], rng.integers(0, 4, (N, 8, 16, C)), 3)
    plain = np.where(rng.random(plain.shape) < 0.25, rng.integers(0, W, plain.shape), plain)
    hs = rng.permutation(W)[:W // 8]; plain[:, 5] = hs[rng.integers(0, W // 8, (N, 16, C))]; plain[:, 5, int(rng.integers(0, K))] = hs[0]
    true = rng.integers(0, W, (N, 8, C)); ct = (plain + true[:, :, None, :]) & M
    a = np.where(rng.random(a.shape) < 0.5, true, a)
    a[:, 5] = true[:, 5]; a[0::2, 5] = (true[0::2, 5] + rng.integers(1, W, true[0::2, 5].shape)) & M
    hot = np.zeros((8, W), bool); hot[np.arange(8)[:, None], words.reshape(8, -1)] = True
    hot[5] = False; hot[5, hs] = True
    bk = np.where(hot[None, :, None, :], rng.integers(7, 16, bk.shape), rng.integers(0, 4, bk.shape))
    th = rng.integers(300, 1700, th.shape); th[:, 7] = 4095
    return pack(ct, bk, pr, pg, a, th)
def setup_inputs_spread(rng):
    ct, bk, pr, pg, a, th = parts(rng)
    ex = rng.choice(np.array([0.2, 1.0, 4.0, 12.0]), (N, 8, 1, W)) * rng.choice(np.array([0.5, 1.0, 2.0]), (N, 8, 16, 1))
    bk = np.minimum((16 * rng.random((N, 8, 16, W)) ** ex).astype(np.int64), 15)
    pr = np.minimum(np.exp2(8 * rng.random((N, 8, 16, C))).astype(np.int64) - 1, 240)
    ct = (ct[:, :, :1] + (np.exp2(12 * rng.random((N, 8, 1, C))) * rng.random((N, 8, 16, C))).astype(np.int64)) & M
    pg = (C * rng.random((N, 8, C)) ** rng.choice(np.array([1.0, 3.0, 8.0]), (N, 8, 1))).astype(np.int64) % C
    th = np.minimum(np.exp2(12 * rng.random((N, 8, C))).astype(np.int64) - 1, 4095)
    return pack(ct, bk, pr, pg, a, th)
def check_inputs(d):
    bad = []
    for k, lo, hi in (("ct", 0, W - 1), ("pr", 0, 240), ("pg", 0, C - 1), ("a0", 0, W - 1), ("th", 0, 4095)):
        if np.min(d[k]) < lo or np.max(d[k]) > hi: bad.append("range of " + k)
    b = np.asarray(d["bk"]).astype(np.float32)
    if np.any(b != np.floor(b)): bad.append("bk holds whole numbers")
    if np.min(b) < 0 or np.max(b) > 15: bad.append("range of bk")
    return bad
def worth(b, s, cap):
    w = np.zeros(cap.shape, np.int32)
    for i in range(16): w = w + np.take_along_axis(b, s[:, :, i:i + 1], 3)
    return np.add.reduce(np.minimum(w, cap), axis=2)
def reference(ct, bk, pr, pg, a0, th):
    x = ct.astype(np.int64).reshape(N, 8, 16, C); cap = pr.astype(np.int32).reshape(N, 8, 16, C)
    b = bk.astype(np.float32).astype(np.int32).reshape(N, 8, 16, W); a = a0.astype(np.int64)
    f = np.stack([gentries(e) for e in pg]).astype(np.int64)
    for t in range(RO):
        s = (x - a[:, :, None, :]) & M
        other = s[[(r + 1 + t % (N - 1)) % N for r in range(N)]]
        z = np.take_along_axis(other, f[:, :, None, :], 3)
        v = worth(b, s, cap); best = a
        for k in range(1, K + 1):
            i = K * t + k - 1
            ak = (x[:, :, i] - z[:, :, i]) & M
            vk = worth(b, (x - ak[:, :, None, :]) & M, cap)
            best = np.where(vk > v, ak, best); v = np.maximum(v, vk)
        a = best
        s = (x - a[:, :, None, :]) & M
        got = np.take_along_axis(b, s.transpose(0, 1, 3, 2).reshape(N, 8, 1, W), 3)
        on = np.repeat(v >= th, 16, axis=2)[:, :, None, :]
        b = np.where(on, b + np.sign(got - b), b)
    return {"ya": a.astype(np.float32), "yv": v.astype(np.float32), "yb": b.reshape(N, 128, W).astype(np.float32).astype(BF)}

from concourse.bass import DstId, RemoteDMATransfer
from concourse.mybir import AluOpType as Op, ActivationFunctionType as Fn

RO, W, C = 5, 2048, 128
PAR = {"c": 64, "v": 134, "h": 64, "v0": 68, "dS": 64}

SCRATCH = {}
for _d, _l in (
        ("int32", "xi:128 a8:128 th8:128 pri:128 pgi:8 key:256 ya1:128 ya2:128 yv1:128"),
        ("float32", "xf:128 a8f:128 t8:128 thk8:128 thn8:128 io8:128 pcol:8 thk:128 onef:384 ex:128 k0:128 k0l:128 "
                    "r1:256 r2:256 yaf:128 yvf:128"),
        ("float16", "xh:384 oneh:384 idh:128 sel:1920 yy:128"),
        ("uint16", "fo:8 ok:256 o3:384"),
        ("bfloat16", "cap:384 oneb:128 idn:128 nid:128 id2k:128 bo:128 bo26:128 cst:512 neg:512 under:1920 over:384 "
                     "book0:4096 book1:4096 gat:8192 mm:512 ww:1024 sg:1024 dd:2048 up:2048")):
    for _e in _l.split():
        SCRATCH[_e.split(":")[0]] = ("sbuf", [128, int(_e.split(":")[1])], _d)
for _t in range(RO + 1):
    SCRATCH["sk%d" % _t] = ("sbuf", [128, 256], "int32")
for _t in range(RO):
    SCRATCH["land%d" % _t] = ("sbuf", [128, C], "int32")
PSUM = ("pS1", "pS2", "pKA", "pKB", "pD0", "pD1", "pU0", "pU1")
for _n in PSUM:
    SCRATCH[_n] = ("psum", [128, 512], "float32")

SEMAPHORES = (["cv", "cs", "cp", "cg", "snd", "sto"] + ["ld%d" % _i for _i in range(32)]
              + ["arr%d" % _t for _t in range(RO)] + ["rel%d" % _t for _t in range(RO)])


def bits(engs):
    return sum(1 << e for e in engs)


def legs(T, topo, t, q):
    n = len(T.cores)
    src, dst = T.cores[q], T.cores[(q - 1 - t % (n - 1)) % n]
    cut = C // 2 if t == 0 else C - PAR["c"]
    if topo.may_write(src, dst):
        e = topo.engines(src, dst)
        if t == 0:
            return [(0, C, dst, e, dst)]
        return [(0, cut, dst, e, dst), (cut, C, dst, e, dst)]
    rel = [c for c in topo.cores_of(src) if topo.die(c) == topo.die(dst) and topo.may_write(c, dst)]
    out = []
    for j, (lo, hi) in enumerate(((0, cut), (cut, C))):
        e = topo.engines(src, rel[j])
        if t == 0:
            e = e[j * len(e) // 2:(j + 1) * len(e) // 2]
        out.append((lo, hi, rel[j], e, dst))
    return out


def relay_program(g, core, T, topo):
    sent = 0
    for t in range(RO):
        for q in range(len(T.cores)):
            for lo, hi, stop, e, dst in legs(T, topo, t, q):
                if stop != core or stop == dst:
                    continue
                land = T["land%d" % t]
                g.wait_ge(T.sem["rel%d" % t], len(e))
                e2 = topo.engines(core, dst)
                rid, pid = topo.addr(dst, core)
                g.remote_dma(land[:, lo:hi], land[:, lo:hi], T.sem["arr%d" % t], T.sem.snd, pid, rid, bits(e2))
                sent += len(e2)
    if sent:
        g.wait_ge(T.sem.snd, sent)


def rank_program(g, core, T, topo):
    rank = T.rank_of(core)
    if rank is None:
        relay_program(g, core, T, topo)
        return
    n = len(T.cores)
    Q = {"g": g, "v": g.vector, "s": g.scalar, "p": g.tensor, "y": g.sync}
    CNT = {"g": "cg", "v": "cv", "s": "cs", "p": "cp"}
    total = {}
    known = {k: {} for k in Q}
    log = {}

    def need(q, sem, val, know=None):
        if known[q].get(sem, 0) >= val:
            return
        Q[q].wait_ge(T.sem[sem], val)
        known[q][sem] = val
        for s, v in (know or {}).items():
            if known[q].get(s, 0) < v:
                known[q][s] = v

    def op(q, call, reads, writes, sem=None, inc=1):
        deps = []
        for regs, w in ((reads, False), (writes, True)):
            for b, lo, hi in regs:
                for q0, l0, h0, w0, s0, v0, k0 in log.get(b, ()):
                    hit = (w or w0) and lo < h0 and l0 < hi
                    if b in PSUM:
                        hit = (q0 != q) or (hit and q != "p")
                    if hit:
                        deps.append((s0, v0, k0))
        deps.sort(key=lambda d: -d[1])
        for s0, v0, k0 in deps:
            need(q, s0, v0, k0)
        ins = call()
        sem = sem or CNT[q]
        total[sem] = total.get(sem, 0) + inc
        if ins is not None:
            ins.then_inc(T.sem[sem], inc)
        know = dict(known[q])
        for regs, w in ((reads, False), (writes, True)):
            for b, lo, hi in regs:
                old = log.get(b, [])
                if w:
                    old = [r for r in old if not (lo <= r[1] and r[2] <= hi)]
                log[b] = old + [(q, lo, hi, w, sem, total[sem], know)]

    def A(r, p=None):
        b, lo, hi = r
        return T[b][:, lo:hi] if p is None else T[b][p[0]:p[1], lo:hi]

    def ind(win, off):
        return A(win).indirect(A(off))

    V, S, PE = g.vector, g.scalar, g.tensor

    def tt(o, a, b, alu, p=None):
        op("v", lambda: V.tensor_tensor(A(o, p), A(a, p), A(b, p), alu), [a, b], [o])

    def ts(o, a, s1, s2, o0, o1=None, p=None, extra=()):
        if o1 is None:
            op("v", lambda: V.tensor_scalar(A(o, p), A(a, p), s1, None, o0), [a] + list(extra), [o])
        else:
            op("v", lambda: V.tensor_scalar(A(o, p), A(a, p), s1, s2, o0, o1), [a] + list(extra), [o])

    def low(o, a):
        ts(o, a, W - 1, None, Op.bitwise_and)

    def cp(o, a, p=None):
        op("v", lambda: V.tensor_copy(A(o, p), A(a, p)), [a], [o])

    def ms(o, val, p=None):
        op("v", lambda: V.memset(A(o, p), val), [], [o])

    def act(o, a, fn, scale=1.0, bias=0.0):
        op("s", lambda: S.activation(A(o), A(a), fn, bias=bias, scale=scale), [a], [o])

    def gather(q, o, win, off):
        if q == "v":
            op("v", lambda: V.tensor_copy(A(o), ind(win, off)), [win, off], [o])
        else:
            op("s", lambda: S.activation(A(o), ind(win, off), Fn.Identity), [win, off], [o])

    def gop(o, win, off, b, alu):
        op("v", lambda: V.tensor_tensor(A(o), ind(win, off), A(b), alu), [win, off, b], [o])

    def mm(o, l, r, start, stop, p=None):
        op("p", lambda: PE.matmul(A(o), A(l, p), A(r, p), start, stop), [l, r], [o])

    def pick(o, a, pattern, base, p=None):
        op("g", lambda: g.affine_select(A(o, p), A(a, p), pattern, Op.is_equal, 0.0, base, 1), [a], [o])

    P8, P64 = (0, 8), (0, 64)
    XI, XF, YY = ("xi", 0, C), ("xf", 0, C), ("yy", 0, C)
    EX, BO, ONE, NID, IDN, IDH = (("ex", 0, 128), ("bo", 0, 128), ("oneb", 0, 128), ("nid", 0, 128), ("idn", 0, 128),
                                  ("idh", 0, 128))

    def sums(o, lo, hi):
        def call():
            ins = None
            for i in range(16):
                ins = PE.matmul(A(o), A(IDN), T.gat[:, 16 * lo + i:16 * hi:16], i == 0, i == 15)
            return ins
        op("p", call, [IDN, ("gat", 16 * lo, 16 * hi)], [o])

    nld = [0]

    def load(q, o, src, p=None, reads=()):
        op(q, lambda: Q[q].dma_start(A(o, p), src), list(reads), [o], sem="ld%d" % nld[0], inc=16)
        nld[0] += 1

    def store(q, dst, src_ap, r):
        op(q, lambda: Q[q].dma_start(dst, src_ap), [r], [], sem="sto", inc=16)

    c, dS = PAR["c"], PAR["dS"]
    cA = C - c

    def send(t, which):
        ls = [l for j, l in enumerate(legs(T, topo, t, rank)) if j in which]
        kb, land = "sk%d" % t, T["land%d" % t]
        tr = []
        for lo, hi, stop, e, dst in ls:
            rid, pid = topo.addr(stop, core)
            sem = T.sem[("arr%d" if stop == dst else "rel%d") % t]
            tr.append((lo, hi, rid, pid, sem, e))
        regs = [(kb, cA + lo, cA + hi) for lo, hi, _, _, _, _ in tr]
        cnt = sum(len(x[5]) for x in tr)

        def call():
            if len(tr) == 1:
                lo, hi, rid, pid, sem, e = tr[0]
                g.remote_dma(land[:, lo:hi], A(regs[0]), sem, T.sem.snd, pid, rid, bits(e))
            else:
                g.remote_dma_fused([RemoteDMATransfer(dst_ids=[DstId(rid=rid, pnc=pid)], dma_engine_mask=bits(e),
                                                      remote_sem=sem, src=A(regs[j]), dst=land[:, lo:hi])
                                    for j, (lo, hi, rid, pid, sem, e) in enumerate(tr)], local_sem=T.sem.snd)
        op("g", call, regs, [], sem="snd", inc=cnt)

    def arrivals(t):
        q = (rank + 1 + t % (n - 1)) % n
        return sum(len(e) if stop == dst else len(topo.engines(stop, dst)) for _, _, stop, e, dst in legs(T, topo, t, q))

    load("y", ("a8", 0, C), T.a0[:, :], P8)
    load("s", XI, T.ct[:, :])
    load("y", ("pgi", 0, 8), T.pg[:, :])
    load("s", ("pri", 0, C), T.pr[:, :])
    load("y", ("th8", 0, C), T.th[:, :], P8)
    load("y", ("book0", 0, W), T.bk[:, :])
    ms(("onef", 0, 384), 1.0)
    cp(("oneh", 0, 384), ("onef", 0, 384))
    ms(ONE, 1.0)

    def selmat(t):
        pick(("sel", 384 * t, 384 * t + 384), ("oneh", 0, 384), [[-1, 3], [-16, 8], [0, 16]], -3 * t)

    pick(EX, ("onef", 0, 128), [[-1, 8], [0, 16]], 0, P8)
    selmat(0)
    pick(IDN, ONE, [[-1, 128]], 0)
    ms(("cst", 0, 512), -491520.0, (0, 32))
    ms(("neg", 0, 512), -1.0 / 64, P64)
    mm(("pKA", 0, 128), EX, EX, True, True, P8)
    cp(("a8f", 0, C), ("a8", 0, C), P8)
    mm(("pS1", 0, C), EX, ("a8f", 0, C), True, True, P8)
    tt(("key", cA, cA + C), XI, ("pS1", 0, C), Op.subtract)
    low(("sk0", cA, cA + C), ("key", cA, cA + C))
    send(0, (0, 1))
    cp(("ok", cA, cA + C), ("sk0", cA, cA + C))
    cp(XF, XI)
    for k in range(4):
        ms(("cst", 128 * k, 128 * k + 128), float(64 * (3 - k)), (32, 64))
    cp(("xh", 0, 128), XF)
    cp(("fo", 0, 8), ("pgi", 0, 8))
    cp(("xh", 128, 256), ("xh", 0, 128))
    cp(("xh", 256, 384), ("xh", 0, 128))
    act(BO, ("pKA", 0, 128), Fn.Copy, 8192.0)
    act(("bo26", 0, 128), ("pKA", 0, 128), Fn.Copy, float(2 ** 26))
    act(NID, IDN, Fn.Copy, -1.0)
    act(("id2k", 0, 128), IDN, Fn.Copy, float(W))
    pick(IDH, ("oneh", 0, 128), [[-1, 128]], 0)
    op("g", lambda: g.iota(T.io8[0:8, :], [[16, C]], -1921 * 8192 + 6144, -16, allow_small_or_imprecise_dtypes=True),
       [], [("io8", 0, C)])
    op("g", lambda: g.iota(T.pcol[:, 0:1], [[0, 1]], 0, 1, allow_small_or_imprecise_dtypes=True), [], [("pcol", 0, 1)])
    for t in range(1, RO):
        selmat(t)
    cp(("cap", 0, 128), ("pri", 0, C))
    ts(("t8", 0, C), ("th8", 0, C), 3841.0, 8192.0, Op.min, Op.mult, P8)
    cp(("cap", 128, 256), ("cap", 0, 128))
    cp(("cap", 256, 384), ("cap", 0, 128))
    ts(("thn8", 0, C), ("t8", 0, C), -4096.0, -8192.0, Op.add, Op.mult, P8)
    tt(("thk8", 0, C), ("t8", 0, C), ("io8", 0, C), Op.add, P8)
    mm(("pS2", 0, C), EX, ("thk8", 0, C), True, True, P8)

    def SEL(t, k):
        return ("sel", 384 * t + 128 * k, 384 * t + 128 * k + 128)

    def wraps(t):
        b = ("pKB", "pD1", "pKA")[t % 3]
        for k in range(3):
            mm((b, 128 * k, 128 * k + 128), SEL(t, k), ("xh", 0, C), True, True)
        tt(("under", 384 * t, 384 * t + 384), ("xh", 0, 384), (b, 0, 384), Op.is_lt)

    def own(t, o, lo, hi):
        mm(o, IDH, ("xh", lo, hi), True, False)
        mm(o, ("id2k", 0, 128), ("under", 384 * t + lo, 384 * t + hi), False, False)

    def spread(t, o, lo, hi, stop):
        cuts = [lo] + [x for x in (128, 256) if lo < x < hi] + [hi]
        for a, b in zip(cuts, cuts[1:]):
            mm((o[0], o[1] + a - lo, o[1] + b - lo), SEL(t, a // 128), ("yy", a % 128, (b - 1) % 128 + 1), False,
               stop and b == hi)

    def keybase(t, o, lo, hi):
        own(t, o, lo, hi)
        spread(t, o, lo, hi, False)
        mm(o, IDN, ("over", lo, hi), False, False)
        mm(o, ONE, ("cst", C + lo, C + hi), False, False, P64)

    T1, T23 = ("pS1", 0, 128), ("pD0", 0, 256)
    K12, K3A, K3B = ("pKA", 0, 256), ("pKB", 0, cA), ("pD1", 0, c)
    ssegs = [(0, dS // 4 * 2), (dS // 4 * 2, dS)]
    useg = [(dS, (dS + C) // 2), ((dS + C) // 2, C)]
    UB = [("pU%d" % j, 0, 16 * (hi - lo)) for j, (lo, hi) in enumerate(useg)]
    DB = [("pD%d" % j, 0, 16 * (hi - lo)) for j, (lo, hi) in enumerate(ssegs)]

    for t in range(RO):
        old, new = "book%d" % (t % 2), "book%d" % ((t + 1) % 2)
        BK, BK2 = (old, 0, W), (old, 0, 2 * W)
        so, sn = "sk%d" % t, "sk%d" % (t + 1)
        last = t == RO - 1
        v, v0 = PAR["v"], (0 if t == 0 else PAR["v0"])
        gather("s", ("gat", 16 * v0, W), BK, ("ok", cA + v0, cA + C))
        act(("up", 16 * dS, W), (old, 16 * dS, W), Fn.Identity, bias=1.0)
        if t == 0:
            wraps(0)
            ts(("thk", 0, C), ("pS2", 0, C), T.pcol[:, 0:1], None, Op.add, extra=[("pcol", 0, 1)])
            cp((old, W, 2 * W), BK)
        else:
            gather("v", ("gat", 0, 16 * v0), BK, ("ok", cA, cA + v0))
        own(t, T1, 0, 128)
        own(t, T23, 128, 384)
        for j, (lo, hi) in enumerate(useg):
            mm(UB[j], IDN, (old, 16 * lo, 16 * hi), True, False)
            mm(UB[j], ONE, ("neg", 0, 16 * (hi - lo)), False, True, P64)
        if t == 0:
            for u in range(1, RO):
                wraps(u)
        need("v", "arr%d" % t, arrivals(t))
        gop(YY, ("land%d" % t, 0, C), ("fo", 0, 8), XI, Op.subtract)
        spread(t, T1, 0, 128, True)
        spread(t, T23, 128, 384, True)
        sums(("pS2", 0, C), 0, C)
        cp(("o3", 0, 128), T1)
        cp(("o3", 128, 384), T23)

        def gat3(q, lo, hi):
            gather(q, ("gat", 16 * (C + lo), 16 * (C + hi)), BK2, ("o3", lo, hi))

        h = 128 + PAR["h"]
        gat3("s", 0, 64)
        gat3("s", 64, 128)
        gat3("v", 128, h)
        ts(("over", 0, 384), ("o3", 0, 384), float(W), -float(W), Op.is_ge, Op.mult)
        mm(("pD1", 0, C), EX, ("thn8", 0, C), True, False, P8)
        mm(("pD0", 0, C), ONE, ("cst", 0, C), True, False, P64)
        tt(("mm", 0, C), ("pS2", 0, C), ("cap", 0, C), Op.min)
        sums(("pS1", 0, 64), C, C + 64)
        sums(("pS1", 128, h), C + 128, C + h)
        mm(("pD0", 0, C), BO, ("mm", 0, C), False, True)
        mm(("pD1", 0, C), ("bo26", 0, 128), ("mm", 0, C), False, True)
        keybase(t, K12, 0, 256)
        gat3("v", h, 128 + v)
        if v < 128:
            gat3("s", 128 + v, 256)
        gat3("s", max(256, 128 + v), 256 + cA)
        gat3("s", 256 + cA, 384)
        sums(("pS1", 64, 128), C + 64, C + 128)
        sums(("pS1", h, 256), C + h, C + 256)
        keybase(t, K3A, 256, 256 + cA)
        K0, K0L = ("k0", 0, C), ("k0l", 0, C)
        tt(K0, ("pD0", 0, C), (so, cA, cA + C), Op.add)
        tt(("pD1", 0, C), ("pD1", 0, C), K0, Op.min)
        tt(K0L, ("pD1", 0, C), ("thk", 0, C), Op.max)
        tt(("mm", C, C + 256), ("pS1", 0, 256), ("cap", 0, 256), Op.min)
        mm(K12, BO, ("mm", C, 3 * C), False, True)
        sums(("pS2", 0, cA), C + 256, C + 256 + cA)
        keybase(t, K3B, 256 + cA, 384)
        tt(("r1", 0, C), ("pKA", 0, C), K0, Op.max)
        tt(("r1", C, 2 * C), ("pKA", 0, C), K0L, Op.max)
        tt(("r2", 0, C), ("pKA", C, 2 * C), ("r1", 0, C), Op.max)
        tt(("r2", C, 2 * C), ("pKA", C, 2 * C), ("r1", C, 2 * C), Op.max)
        tt(("mm", 384, 384 + cA), ("pS2", 0, cA), ("cap", 256, 256 + cA), Op.min)
        mm(K3A, BO, ("mm", 384, 384 + cA), False, True)
        sums(("pS1", 0, c), C + 256 + cA, C + 384)
        tt(("key", cA, 2 * cA), K3A, ("r2", 0, cA), Op.max)
        tt(("key", 0, cA), K3A, ("r2", C, C + cA), Op.max)
        low((sn, 0, 2 * cA), ("key", 0, 2 * cA))
        if not last:
            send(t + 1, (0,))
        cp(("ok", 0, 2 * cA), (sn, 0, 2 * cA))
        tt(("mm", 512 - c, 512), ("pS1", 0, c), ("cap", 384 - c, 384), Op.min)
        mm(K3B, BO, ("mm", 512 - c, 512), False, True)
        tt(("key", 2 * cA, cA + C), K3B, ("r2", cA, C), Op.max)
        tt(("key", cA + C, 256), K3B, ("r2", C + cA, 2 * C), Op.max)
        if not last:
            low((sn, 2 * cA, cA + C), ("key", 2 * cA, cA + C))
            send(t + 1, (1,))
        low((sn, cA + C, 256), ("key", cA + C, 256))
        b0 = cA + C if last else 2 * cA
        cp(("ok", b0, 256), (sn, b0, 256))

        def lofs(lo, hi):
            out = []
            if lo < cA:
                out.append((lo, min(hi, cA), 0))
            if hi > cA:
                out.append((max(lo, cA), hi, C))
            return out

        def keep(lo, hi):
            r = (new, 16 * lo, 16 * hi)
            if last:
                store("y", T.yb[:, 16 * lo:16 * hi], A(r), r)
            else:
                load("y", (new, W + 16 * lo, W + 16 * hi), A(r), reads=[r])

        for j, (lo, hi) in enumerate(ssegs):
            for a, b, sh in lofs(lo, hi):
                gather("s", ("ww", 16 * a, 16 * b), BK, ("ok", a + sh, b + sh))
            mm(DB[j], NID, (old, 16 * lo, 16 * hi), True, False)
            mm(DB[j], IDN, ("ww", 16 * lo, 16 * hi), False, True)
        for j, (lo, hi) in enumerate(ssegs):
            act(("sg", 16 * lo, 16 * hi), DB[j], Fn.Sign)
            mm(DB[j], IDN, (old, 16 * lo, 16 * hi), True, False)
            mm(DB[j], IDN, ("sg", 16 * lo, 16 * hi), False, True)
        for lo, hi in useg:
            for a, b, sh in lofs(lo, hi):
                gop(("dd", 16 * a, 16 * b), BK, ("ok", a + sh, b + sh), ("up", 16 * a, 16 * b), Op.min)
        for j in range(2):
            lo, hi = useg[j]
            tt((new, 16 * lo, 16 * hi), UB[j], ("dd", 16 * lo, 16 * hi), Op.max)
            keep(lo, hi)
            act((new, 16 * ssegs[j][0], 16 * ssegs[j][1]), DB[j], Fn.Copy)
            keep(*ssegs[j])

    KE = ("key", cA, cA + C)
    tt(("ya1", 0, C), XI, KE, Op.subtract)
    ts(("yv1", 0, C), KE, 13, None, Op.arith_shift_right)
    low(("ya2", 0, C), ("ya1", 0, C))
    ts(("yvf", 0, C), ("yv1", 0, C), 1920.0, None, Op.add)
    cp(("yaf", 0, C), ("ya2", 0, C))
    store("s", T.yv[:, :], T.yvf[0:128:16, :], ("yvf", 0, C))
    store("s", T.ya[:, :], T.yaf[0:128:16, :], ("yaf", 0, C))
    for sem, val in total.items():
        need("g", sem, val)
